import numpy as np
import ml_dtypes


def mxq(x, axis, fmt="e4m3"):
    dtype, down = {"e4m3": (ml_dtypes.float8_e4m3fn, 7), "e5m2": (ml_dtypes.float8_e5m2, 14)}[fmt]
    v = np.moveaxis(np.asarray(x, np.float32).astype(ml_dtypes.bfloat16).astype(np.float64), axis, -1)
    blocks = v.reshape(v.shape[:-1] + (-1, 32))
    amax = np.abs(blocks).max(-1, keepdims=True)
    byte = np.maximum(np.where(amax > 0, np.frexp(amax)[1] - 1 + 127, 0) - down, 1)
    scale = np.exp2(byte - 127.0)
    codes = (blocks / scale).astype(np.float32).astype(dtype).astype(np.float64)
    return np.moveaxis((codes * scale).reshape(v.shape), -1, axis)


WIDE = False


def mx_kscale(k):
    if not WIDE:
        return np.ones(k)
    levels = np.array([10, -10, 5, -5, 0])
    if k % 512:
        return np.exp2(np.random.permutation(np.resize(levels, k // 32))).repeat(32)
    a = np.empty((k // 512, 16))
    for p in range(k // 512):
        a[p, :8] = np.random.permutation(np.resize(levels, 8))
        for g in range(8):
            far = levels[np.abs(levels - a[p, g]) >= 10]
            a[p, g + 8] = far[np.random.randint(len(far))]
    return np.exp2(a.ravel()).repeat(32)


def f64(x):
    return np.asarray(x).astype(np.float64)


def striped(idx):
    return np.tile(idx.reshape(-1, 16).T, (8, 1)).astype(np.uint16)


def unstriped(offs):
    return offs[:16].T.reshape(-1).astype(np.int64)


def striped8(idx):
    return np.concatenate([x.reshape(-1, 16).T for x in idx]).astype(np.uint16)


def runs(offs, k):
    lists = np.stack([offs[16 * r : 16 * r + 16].T.reshape(-1) for r in range(8)]).astype(np.int64)
    return lists[np.arange(k) % 512 // 64]


def pack_weight(w):
    k, n = w.shape
    w = f64(np.asarray(w, np.float32).astype(ml_dtypes.bfloat16)).reshape(k // 32, 32, n)
    amax = np.abs(w).max(1)
    byte = np.clip(np.where(amax > 0, np.frexp(amax)[1] - 1 + 127 - 7, 1), 1, 254)
    scaled = (w * np.exp2(127.0 - byte)[:, None, :]).reshape(k, n).astype(np.float32)
    words = np.ascontiguousarray(scaled.reshape(k // 512, 128, 4, n).transpose(0, 1, 3, 2)).astype(ml_dtypes.float8_e4m3fn).view(np.uint8)
    return words, np.ascontiguousarray(byte.astype(np.uint8).reshape(k // 512, 16, n))


def unpack_weight(words, scales):
    g, p, n, _ = words.shape
    vals = np.ascontiguousarray(words).view(ml_dtypes.float8_e4m3fn).astype(np.float64) * np.repeat(np.exp2(scales.astype(np.float64) - 127.0), 8, axis=1)[..., None]
    return vals.transpose(0, 1, 3, 2).reshape(g * 512, n)


E2M1 = np.array([0.0, 0.5, 1.0, 1.5, 2.0, 3.0, 4.0, 6.0, -0.0, -0.5, -1.0, -1.5, -2.0, -3.0, -4.0, -6.0])


def pack_fp4(w):
    k, n = w.shape
    w = f64(np.asarray(w, np.float32).astype(ml_dtypes.bfloat16)).reshape(k // 32, 32, n)
    amax = np.abs(w).max(1)
    mant, ex = np.frexp(amax / 6.0)
    byte = np.clip(np.where(amax > 0, np.where(mant > 0.5, ex, ex - 1) + 127, 1), 1, 254)
    scaled = (w * np.exp2(127.0 - byte)[:, None, :]).reshape(k, n).astype(np.float32)
    c = np.ascontiguousarray(scaled.reshape(k // 512, 128, 4, n).transpose(0, 1, 3, 2)).astype(ml_dtypes.float4_e2m1fn).view(np.uint8) & 0xF
    words = (c[..., 0::2] | (c[..., 1::2] << 4)).reshape(k // 512, 128, 2 * n)
    return np.ascontiguousarray(words), np.ascontiguousarray(byte.astype(np.uint8).reshape(k // 512, 16, n))


def unpack_fp4(words, scales):
    g, _, n = scales.shape
    words = np.ascontiguousarray(words).reshape(g, 128, n, 2)
    nib = np.empty((g, 128, n, 4), np.uint8)
    nib[..., 0::2] = words & 0xF
    nib[..., 1::2] = words >> 4
    vals = E2M1[nib] * np.repeat(np.exp2(scales.astype(np.float64) - 127.0), 8, axis=1)[..., None]
    return vals.transpose(0, 1, 3, 2).reshape(g * 512, n)


def sigmoid(v):
    return 1.0 / (1.0 + np.exp(-np.maximum(v, -700.0)))

def planes(y):
    n, m = y.shape
    v = y.astype(np.float32).astype(ml_dtypes.bfloat16).astype(np.float64).reshape(n // 32, 32, m)
    top = np.abs(v).max(1)
    byte = np.clip(np.where(top > 0, np.frexp(top)[1] - 1 + 127 - 7, 1), 1, 254)
    codes = (v * np.exp2(127.0 - byte)[:, None, :]).reshape(n, m).astype(np.float32).astype(ml_dtypes.float8_e4m3fn).view(np.uint8)
    words = codes.reshape(n // 512, 128, 4, m).transpose(0, 1, 3, 2)
    return np.ascontiguousarray(words), np.ascontiguousarray(byte.astype(np.uint8).reshape(n // 512, 16, m))


K, T, S, N, H, U = 512, 2048, 512, 512, 512, 1024


def setup_inputs():
    n = np.random.standard_normal
    s = mx_kscale(K)[:, None]
    u = mx_kscale(H)
    packed_xT = pack_weight(n((K, T)) * s)
    packed_w1 = pack_fp4(n((K, H)) / np.sqrt(K) / s)
    packed_w2 = pack_fp4(n((K, H)) / np.sqrt(K) / s)
    packed_w3 = pack_fp4(n((H, N)) / np.sqrt(H) / u[:, None])
    return {
        "x_words": packed_xT[0],
        "x_scales": packed_xT[1],
        "w1_words": packed_w1[0],
        "w1_scales": packed_w1[1],
        "w2_words": packed_w2[0],
        "w2_scales": packed_w2[1],
        "beta": np.repeat(np.random.uniform(0.5, 1.5, (8, S)), 64, axis=0).astype(np.float32),
        "gn": (np.random.uniform(0.5, 1.5, (H, 1)) * u[:, None]).astype(np.float32),
        "w3_words": packed_w3[0],
        "w3_scales": packed_w3[1],
        "mem": n((N, U)).astype(np.float32),
        "offs": striped(np.random.permutation(T)[:S]),
        "two": striped(np.random.permutation(T)[:S]),
        "e1": striped8(np.stack([np.random.permutation(S) for _ in range(8)])),
        "e2": striped8(np.stack([np.random.permutation(S) for _ in range(8)])),
        "slot": striped8(np.stack([np.random.permutation(U)[:S] for _ in range(8)])),
    }


def reference(x_words, x_scales, w1_words, w1_scales, w2_words, w2_scales, beta, gn, w3_words, w3_scales, mem, offs, two, e1, e2, slot):
    xq = unpack_weight(x_words, x_scales)[:, unstriped(offs)]
    y = sigmoid(unpack_fp4(w1_words, w1_scales).T @ xq)
    x_two = unpack_weight(x_words, x_scales)[:, unstriped(two)]
    c = sigmoid(unpack_fp4(w2_words, w2_scales).T @ x_two)
    nw = (f64(beta) * y) * (c[np.arange(H)[:, None], runs(e1, H)] + c[np.arange(H)[:, None], runs(e2, H)])
    z = f64(gn) * (nw - (0.75 * c))
    h = unpack_fp4(w3_words, w3_scales).T @ mxq(z, 0, "e4m3")
    out = f64(mem).copy()
    out[np.arange(N)[:, None], runs(slot, N)] = h
    return (out,) + planes(out)

@@ -1,0 +1,263 @@
+from contextlib import ExitStack
+
+import concourse.mybir as mybir
+
+K, T, S, N, H, U = 512, 2048, 512, 512, 512, 1024
+FLOPS = 3 * 2 * 512 * 512 * 512
+
+F32 = mybir.dt.float32
+BF16 = mybir.dt.bfloat16
+I32 = mybir.dt.int32
+U32 = mybir.dt.uint32
+U16 = mybir.dt.uint16
+U8 = mybir.dt.uint8
+FP8X4 = mybir.dt.float8_e4m3fn_x4
+FP4X4 = mybir.dt.float4_e2m1fn_x4
+MULT = mybir.AluOpType.mult
+ADD = mybir.AluOpType.add
+SIGMOID = mybir.ActivationFunctionType.Sigmoid
+
+P = 128
+PACK = 4
+BANK = 512
+CHUNKS = [(0, 128, "V"), (128, 128, "S"), (256, 256, "S")]
+TAIL = [(0, 256, "V"), (640, 128, "S"), (256, 256, "V"), (768, 256, "S"), (512, 128, "V")]
+
+
+def tile_picked_sirstep_none_po_kernel(
+    tc, x_words, x_scales, w1_words, w1_scales, w2_words, w2_scales, beta, gn, w3_words, w3_scales,
+    mem, offs, two, e1, e2, slot, out_0, out_1, out_2,
+):
+    nc = tc.nc
+    with ExitStack() as ctx:
+        lists = ctx.enter_context(tc.tile_pool(name="lists", bufs=1))
+        keep = ctx.enter_context(tc.tile_pool(name="keep", bufs=1))
+        ring = ctx.enter_context(tc.tile_pool(name="ring", bufs=2))
+        psum = ctx.enter_context(tc.psum_pool(name="psum", bufs=1))
+        psum2 = ctx.enter_context(tc.psum_pool(name="psum2", bufs=2))
+
+        def load_list(name, src):
+            tile = lists.tile([P, S // 16], U16, name=name)
+            nc.sync.dma_start(tile[:], src)
+            return tile
+
+        def load_scale_rows(tile, src, queue):
+            for q in range(4):
+                queue.dma_start(tile[32 * q : 32 * q + 4, :].bitcast(I32), src[0, 4 * q : 4 * q + 4, :].bitcast(I32))
+
+        def raw_weight(name, words, tags):
+            raw_words = keep.tile([P, 2 * H], U8, name=name + "_raw_words", tag=tags[0], align_bytes=64)
+            raw_scales = keep.tile([P, H], U8, name=name + "_raw_scales", tag=tags[1], align_bytes=64)
+            nc.sync.dma_start(raw_words[:].bitcast(I32), words[0].bitcast(I32))
+            return raw_words, raw_scales
+
+        def deal_words(name, raw_words):
+            dealt = keep.tile([P, 2 * H], U8, name=name + "_words", align_bytes=64)
+            nc.vector.tensor_copy(
+                dealt[:].rearrange("p (t m b) -> p m t b", t=PACK, b=2),
+                raw_words[:].rearrange("p (m t b) -> p m t b", t=PACK, b=2),
+            )
+            return dealt
+
+        def deal_scales(name, raw_scales):
+            dealt = keep.tile([P, H], U8, name=name + "_scales", align_bytes=64)
+            nc.vector.tensor_copy(
+                dealt[:].rearrange("p (t m) -> p m t", t=PACK),
+                raw_scales[:].rearrange("p (m t) -> p m t", t=PACK),
+            )
+            return dealt
+
+        def product(out, w_words, w_scales, t, codes, scales):
+            nc.tensor.matmul_mx(
+                out,
+                lhsT=w_words[:, 2 * P * t : 2 * P * (t + 1)].bitcast(FP4X4),
+                lhsT_scale=w_scales[:, P * t : P * (t + 1)],
+                rhs=codes.bitcast(FP8X4),
+                rhs_scale=scales,
+                start=True,
+                stop=True,
+            )
+
+        warm = keep.tile([P, 1], F32, name="warm")
+        warm_out = keep.tile([P, 1], F32, name="warm_out")
+        nc.gpsimd.memset(warm[:], 0.0)
+        nc.scalar.activation(warm_out[:], warm[:], SIGMOID)
+
+        xs = keep.tile([P, T], U8, name="xs", align_bytes=64)
+        nc.vector.memset(xs[:].bitcast(I32), 0)
+        two_t = load_list("two_t", two)
+        w2_rw, w2_rs = raw_weight("w2", w2_words, ("page0", "page2"))
+        nc.vector.memset(w2_rs[:].bitcast(I32), 0)
+        load_scale_rows(xs, x_scales, nc.sync)
+        xw = keep.tile([P, T], I32, name="xw", align_bytes=64)
+        nc.sync.dma_start(xw[:], x_words[0].rearrange("p n t -> p (n t)").bitcast(I32))
+        load_scale_rows(w2_rs, w2_scales, nc.sync)
+        offs_t = load_list("offs_t", offs)
+        w1_rw, w1_rs = raw_weight("w1", w1_words, ("page1", "page3"))
+        nc.gpsimd.memset(w1_rs[:].bitcast(I32), 0)
+        load_scale_rows(w1_rs, w1_scales, nc.sync)
+        e1_t = load_list("e1_t", e1)
+        e2_t = load_list("e2_t", e2)
+        gain = keep.tile([P, PACK], F32, name="gain")
+        nc.sync.dma_start(gain[:], gn.rearrange("(p t) o -> p (t o)", t=PACK))
+        rate = keep.tile([P, S], F32, name="rate")
+        nc.sync.dma_start(rate[:], beta.rearrange("(p t) s -> p t s", t=PACK)[:, 0, :])
+        w3_rw, w3_rs = raw_weight("w3", w3_words, ("w3_raw_words", "w3_raw_scales"))
+        nc.gpsimd.memset(w3_rs[:].bitcast(I32), 0)
+        load_scale_rows(w3_rs, w3_scales, nc.sync)
+        slot_t = load_list("slot_t", slot)
+
+        def pick(name, list_t, c0, n):
+            words = keep.tile([P, n], I32, name=name + "_words", align_bytes=64)
+            scales = keep.tile([P, n], U8, name=name + "_scales", align_bytes=64)
+            entries = list_t[:, c0 // 16 : (c0 + n) // 16]
+            nc.vector.tensor_copy(scales[:], xs[:].indirect(entries))
+            nc.vector.tensor_copy(words[:].bitcast(U32), xw[:].bitcast(U32).indirect(entries))
+            return words, scales
+
+        w2_w = deal_words("w2", w2_rw)
+        two_words, two_scales = pick("two", two_t, 0, S)
+        w2_s = deal_scales("w2", w2_rs)
+
+        c_banks = [psum.tile([P, BANK], F32, name="c_bank%d" % t) for t in range(PACK)]
+        c_rows = [keep.tile([P, S], F32, name="c_row%d" % t) for t in range(PACK)]
+        u_rows = [keep.tile([P, S], F32, name="u_row%d" % t) for t in range(PACK)]
+        for t in range(PACK):
+            product(c_banks[t][:], w2_w, w2_s, t, two_words[:], two_scales[:])
+            nc.scalar.activation(c_rows[t][:], c_banks[t][:], SIGMOID)
+
+        w1_w = deal_words("w1", w1_rw)
+        w1_s = deal_scales("w1", w1_rs)
+        HALF = S // 2
+        picked = [pick("offs0", offs_t, 0, HALF)]
+        own = keep.tile([P, PACK], F32, name="own")
+        nc.gpsimd.tensor_scalar(own[:], gain[:], -0.75, 0.0, MULT, ADD)
+
+        mem_rows = mem.rearrange("(p t) u -> p t u", t=PACK)
+        pages = []
+        for t in range(PACK):
+            page = keep.tile([P, U], F32, name="page%d" % t, tag="page%d" % t, align_bytes=64)
+            nc.sync.dma_start(page[:], mem_rows[:, t, :])
+            pages.append(page)
+
+        def susceptible(k):
+            c0, n, mode = CHUNKS[k]
+            words, scales = picked[c0 // HALF]
+            cols = slice(c0 % HALF, c0 % HALF + n)
+            y = ring.tile([P, PACK, n], F32, name="y")
+            per_bank = BANK // n
+            for b in range(PACK // per_bank):
+                bank = psum2.tile([P, per_bank, n], F32, name="y_bank")
+                for i in range(per_bank):
+                    product(bank[:, i, :], w1_w, w1_s, b * per_bank + i, words[:, cols], scales[:, cols])
+                nc.scalar.activation(y[:, b * per_bank : (b + 1) * per_bank, :], bank[:], SIGMOID)
+            return y
+
+        def contacts(k):
+            c0, n, mode = CHUNKS[k]
+            first = ring.tile([P, PACK, n], F32, name="first")
+            second = ring.tile([P, PACK, n], F32, name="second")
+            a = e1_t[:, c0 // 16 : (c0 + n) // 16]
+            b = e2_t[:, c0 // 16 : (c0 + n) // 16]
+            for t in range(PACK):
+                if mode == "V":
+                    nc.vector.tensor_copy(first[:, t, :], c_rows[t][:].indirect(a))
+                else:
+                    nc.scalar.activation(first[:, t, :], u_rows[t][:].indirect(a), SIGMOID)
+                if mode == "S":
+                    nc.scalar.activation(second[:, t, :], u_rows[t][:].indirect(b), SIGMOID)
+            if mode != "S":
+                for t in range(PACK):
+                    nc.vector.tensor_tensor(second[:, t, :], c_rows[t][:].indirect(b), first[:, t, :], ADD)
+            return first, second
+
+        def change(k, y, first, second):
+            c0, n, mode = CHUNKS[k]
+            cols = slice(c0, c0 + n)
+            nc.vector.tensor_tensor(y[:], y[:], rate[:, cols].unsqueeze(1).to_broadcast([P, PACK, n]), MULT)
+            if mode == "S":
+                for t in (0, 2):
+                    nc.vector.tensor_tensor(second[:, t : t + 2, :], second[:, t : t + 2, :], first[:, t : t + 2, :], ADD)
+            for t in range(PACK):
+                nc.vector.scalar_tensor_tensor(second[:, t, :], second[:, t, :], gain[:, t : t + 1], y[:, t, :], MULT, MULT)
+            z = ring.tile([P, PACK, n], BF16, name="z")
+            for t in range(PACK):
+                nc.vector.scalar_tensor_tensor(z[:, t, :], c_rows[t][:, cols], own[:, t : t + 1], second[:, t, :], MULT, ADD)
+            grouped = ring.tile([P, n, PACK], BF16, name="grouped", align_bytes=64)
+            if k == len(CHUNKS) - 1:
+                nc.vector.tensor_copy(grouped[:], z[:].rearrange("p t j -> p j t"))
+            else:
+                nc.scalar.copy(grouped[:], z[:].rearrange("p t j -> p j t"))
+            return grouped
+
+        def layer(k, grouped):
+            c0, n, mode = CHUNKS[k]
+            codes = ring.tile([P, n], I32, name="z_codes", align_bytes=64)
+            scales = ring.tile([P, n], U8, name="z_scales", align_bytes=64)
+            nc.vector.quantize_mx(codes[:].bitcast(FP8X4), scales[:], grouped[:].rearrange("p j t -> p (j t)"))
+            h = ring.tile([P, PACK, n], F32, name="h")
+            per_bank = BANK // n
+            for b in range(PACK // per_bank):
+                bank = psum2.tile([P, per_bank, n], F32, name="h_bank")
+                for i in range(per_bank):
+                    product(bank[:, i, :], w3_w, w3_s, b * per_bank + i, codes[:], scales[:])
+                nc.scalar.copy(h[:, b * per_bank : (b + 1) * per_bank, :], bank[:])
+            return h
+
+        out_rows = out_0.rearrange("(p t) u -> p t u", t=PACK)
+        rounded = keep.tile([P, PACK, U], BF16, name="rounded")
+
+        def put(k, h):
+            c0, n, mode = CHUNKS[k]
+            for t in range(PACK):
+                nc.vector.tensor_copy(pages[t][:].indirect(slot_t[:, c0 // 16 : (c0 + n) // 16]), h[:, t, :])
+                if k == len(CHUNKS) - 1:
+                    nc.sync.dma_start(out_rows[:, t, :], pages[t][:])
+                    if t < PACK - 1:
+                        nc.scalar.copy(rounded[:, t, :], pages[t][:])
+
+        y0 = susceptible(0)
+        first0, second0 = contacts(0)
+        for t in range(PACK):
+            nc.scalar.copy(u_rows[t][:], c_banks[t][:])
+        grouped0 = change(0, y0, first0, second0)
+        w3_w = deal_words("w3", w3_rw)
+        w3_s = deal_scales("w3", w3_rs)
+        h_prev = layer(0, grouped0)
+        picked.append(pick("offs1", offs_t, HALF, HALF))
+        for k in range(1, len(CHUNKS)):
+            first, second = contacts(k)
+            y = susceptible(k)
+            grouped = change(k, y, first, second)
+            if k == len(CHUNKS) - 1:
+                h_next = layer(k, grouped)
+                put(k - 1, h_prev)
+            else:
+                put(k - 1, h_prev)
+                h_next = layer(k, grouped)
+            h_prev = h_next
+        put(len(CHUNKS) - 1, h_prev)
+
+        out_codes = keep.tile([P, U], I32, name="out_codes", align_bytes=64)
+        out_scales = keep.tile([P, U], U8, name="out_scales", align_bytes=64)
+        out_words = out_1[0].rearrange("p n t -> p (n t)").bitcast(I32)
+        last = PACK - 1
+        blocks = []
+        for i, (c0, n, engine) in enumerate(TAIL):
+            cols = slice(c0, c0 + n)
+            block = keep.tile([P, n, PACK], BF16, name="block%d" % i, align_bytes=64)
+            source = rounded[:, :, cols].rearrange("p t j -> p j t")
+            if engine == "V":
+                nc.vector.tensor_copy(rounded[:, last, cols], pages[last][:, cols])
+                nc.vector.tensor_copy(block[:], source)
+            else:
+                nc.scalar.copy(rounded[:, last, cols], pages[last][:, cols])
+                nc.scalar.copy(block[:], source)
+            blocks.append(block)
+        for i, (c0, n, engine) in enumerate(TAIL):
+            cols = slice(c0, c0 + n)
+            nc.vector.quantize_mx(out_codes[:, cols].bitcast(FP8X4), out_scales[:, cols], blocks[i][:].rearrange("p j t -> p (j t)"))
+            nc.sync.dma_start(out_words[:, cols], out_codes[:, cols])
+        for q in range(4):
+            queue = nc.sync if q % 2 == 0 else nc.scalar
+            queue.dma_start(out_2[0, 4 * q : 4 * q + 4, :].bitcast(I32), out_scales[32 * q : 32 * q + 4, :].bitcast(I32))

@@ -16,12 +16,15 @@ FP4X4 = mybir.dt.float4_e2m1fn_x4
 MULT = mybir.AluOpType.mult
 ADD = mybir.AluOpType.add
 SIGMOID = mybir.ActivationFunctionType.Sigmoid
+COPY = mybir.ActivationFunctionType.Copy
 
 P = 128
 PACK = 4
 BANK = 512
-CHUNKS = [(0, 128, "V"), (128, 128, "S"), (256, 256, "S")]
-TAIL = [(0, 256, "V"), (640, 128, "S"), (256, 256, "V"), (768, 256, "S"), (512, 128, "V")]
+CHUNK = 128
+HALF = 256
+SUB = 64
+PIECE = 256
 
 
 def tile_picked_sirstep_none_po_kernel(
@@ -32,18 +35,16 @@ def tile_picked_sirstep_none_po_kernel(
     with ExitStack() as ctx:
         lists = ctx.enter_context(tc.tile_pool(name="lists", bufs=1))
         keep = ctx.enter_context(tc.tile_pool(name="keep", bufs=1))
-        ring = ctx.enter_context(tc.tile_pool(name="ring", bufs=2))
         psum = ctx.enter_context(tc.psum_pool(name="psum", bufs=1))
-        psum2 = ctx.enter_context(tc.psum_pool(name="psum2", bufs=2))
 
         def load_list(name, src):
             tile = lists.tile([P, S // 16], U16, name=name)
             nc.sync.dma_start(tile[:], src)
             return tile
 
-        def load_scale_rows(tile, src, queue):
+        def load_scale_rows(tile, src, queues):
             for q in range(4):
-                queue.dma_start(tile[32 * q : 32 * q + 4, :].bitcast(I32), src[0, 4 * q : 4 * q + 4, :].bitcast(I32))
+                queues[q].dma_start(tile[32 * q : 32 * q + 4, :].bitcast(I32), src[0, 4 * q : 4 * q + 4, :].bitcast(I32))
 
         def raw_weight(name, words, tags):
             raw_words = keep.tile([P, 2 * H], U8, name=name + "_raw_words", tag=tags[0], align_bytes=64)
@@ -51,16 +52,16 @@ def tile_picked_sirstep_none_po_kernel(
             nc.sync.dma_start(raw_words[:].bitcast(I32), words[0].bitcast(I32))
             return raw_words, raw_scales
 
-        def deal_words(name, raw_words):
-            dealt = keep.tile([P, 2 * H], U8, name=name + "_words", align_bytes=64)
+        def deal_words(name, raw_words, tag):
+            dealt = keep.tile([P, 2 * H], U8, name=name + "_words", tag=tag, align_bytes=64)
             nc.vector.tensor_copy(
                 dealt[:].rearrange("p (t m b) -> p m t b", t=PACK, b=2),
                 raw_words[:].rearrange("p (m t b) -> p m t b", t=PACK, b=2),
             )
             return dealt
 
-        def deal_scales(name, raw_scales):
-            dealt = keep.tile([P, H], U8, name=name + "_scales", align_bytes=64)
+        def deal_scales(name, raw_scales, tag):
+            dealt = keep.tile([P, H], U8, name=name + "_scales", tag=tag, align_bytes=64)
             nc.vector.tensor_copy(
                 dealt[:].rearrange("p (t m) -> p m t", t=PACK),
                 raw_scales[:].rearrange("p (m t) -> p m t", t=PACK),
@@ -78,186 +79,191 @@ def tile_picked_sirstep_none_po_kernel(
                 stop=True,
             )
 
-        warm = keep.tile([P, 1], F32, name="warm")
-        warm_out = keep.tile([P, 1], F32, name="warm_out")
-        nc.gpsimd.memset(warm[:], 0.0)
-        nc.scalar.activation(warm_out[:], warm[:], SIGMOID)
+        def held(shape, dtype, name, tag=None):
+            return keep.tile(shape, dtype, name=name, tag=tag or name, align_bytes=64)
 
-        xs = keep.tile([P, T], U8, name="xs", align_bytes=64)
+        def entries(list_t, c0, n):
+            return list_t[:, c0 // 16 : (c0 + n) // 16]
+
+        xs = held([P, T], U8, "xs")
         nc.vector.memset(xs[:].bitcast(I32), 0)
         two_t = load_list("two_t", two)
-        w2_rw, w2_rs = raw_weight("w2", w2_words, ("page0", "page2"))
-        nc.vector.memset(w2_rs[:].bitcast(I32), 0)
-        load_scale_rows(xs, x_scales, nc.sync)
-        xw = keep.tile([P, T], I32, name="xw", align_bytes=64)
+        w2_rw, w2_rs = raw_weight("w2", w2_words, ("w2_rw", "w2_rs"))
+        load_scale_rows(xs, x_scales, (nc.sync,) * 4)
+        xw = held([P, T], I32, "xw")
         nc.sync.dma_start(xw[:], x_words[0].rearrange("p n t -> p (n t)").bitcast(I32))
-        load_scale_rows(w2_rs, w2_scales, nc.sync)
+        nc.vector.memset(w2_rs[:].bitcast(I32), 0)
+        load_scale_rows(w2_rs, w2_scales, (nc.sync,) * 4)
+        warm = held([P, 1], F32, "warm")
+        warm_out = held([P, 1], F32, "warm_out")
+        nc.gpsimd.memset(warm[:], 0.0)
+        nc.scalar.activation(warm_out[:], warm[:], SIGMOID)
         offs_t = load_list("offs_t", offs)
-        w1_rw, w1_rs = raw_weight("w1", w1_words, ("page1", "page3"))
-        nc.gpsimd.memset(w1_rs[:].bitcast(I32), 0)
-        load_scale_rows(w1_rs, w1_scales, nc.sync)
+        w1_rw, w1_rs = raw_weight("w1", w1_words, ("w1_rw", "w1_rs"))
         e1_t = load_list("e1_t", e1)
         e2_t = load_list("e2_t", e2)
-        gain = keep.tile([P, PACK], F32, name="gain")
+        gain = held([P, PACK], F32, "gain")
         nc.sync.dma_start(gain[:], gn.rearrange("(p t) o -> p (t o)", t=PACK))
-        rate = keep.tile([P, S], F32, name="rate")
+        nc.gpsimd.memset(w1_rs[:].bitcast(I32), 0)
+        load_scale_rows(w1_rs, w1_scales, (nc.gpsimd,) * 4)
+        rate = held([P, S], F32, "rate")
         nc.sync.dma_start(rate[:], beta.rearrange("(p t) s -> p t s", t=PACK)[:, 0, :])
-        w3_rw, w3_rs = raw_weight("w3", w3_words, ("w3_raw_words", "w3_raw_scales"))
-        nc.gpsimd.memset(w3_rs[:].bitcast(I32), 0)
-        load_scale_rows(w3_rs, w3_scales, nc.sync)
+        w3_rw, w3_rs = raw_weight("w3", w3_words, ("w3_rw", "w3_rs"))
+        nc.vector.memset(w3_rs[:].bitcast(I32), 0)
+        load_scale_rows(w3_rs, w3_scales, (nc.sync,) * 4)
         slot_t = load_list("slot_t", slot)
-
-        def pick(name, list_t, c0, n):
-            words = keep.tile([P, n], I32, name=name + "_words", align_bytes=64)
-            scales = keep.tile([P, n], U8, name=name + "_scales", align_bytes=64)
-            entries = list_t[:, c0 // 16 : (c0 + n) // 16]
-            nc.vector.tensor_copy(scales[:], xs[:].indirect(entries))
-            nc.vector.tensor_copy(words[:].bitcast(U32), xw[:].bitcast(U32).indirect(entries))
-            return words, scales
-
-        w2_w = deal_words("w2", w2_rw)
-        two_words, two_scales = pick("two", two_t, 0, S)
-        w2_s = deal_scales("w2", w2_rs)
-
-        c_banks = [psum.tile([P, BANK], F32, name="c_bank%d" % t) for t in range(PACK)]
-        c_rows = [keep.tile([P, S], F32, name="c_row%d" % t) for t in range(PACK)]
-        u_rows = [keep.tile([P, S], F32, name="u_row%d" % t) for t in range(PACK)]
-        for t in range(PACK):
-            product(c_banks[t][:], w2_w, w2_s, t, two_words[:], two_scales[:])
-            nc.scalar.activation(c_rows[t][:], c_banks[t][:], SIGMOID)
-
-        w1_w = deal_words("w1", w1_rw)
-        w1_s = deal_scales("w1", w1_rs)
-        HALF = S // 2
-        picked = [pick("offs0", offs_t, 0, HALF)]
-        own = keep.tile([P, PACK], F32, name="own")
-        nc.gpsimd.tensor_scalar(own[:], gain[:], -0.75, 0.0, MULT, ADD)
-
         mem_rows = mem.rearrange("(p t) u -> p t u", t=PACK)
         pages = []
         for t in range(PACK):
-            page = keep.tile([P, U], F32, name="page%d" % t, tag="page%d" % t, align_bytes=64)
+            page = held([P, U], F32, "page%d" % t)
             nc.sync.dma_start(page[:], mem_rows[:, t, :])
             pages.append(page)
 
-        def susceptible(k):
-            c0, n, mode = CHUNKS[k]
-            words, scales = picked[c0 // HALF]
-            cols = slice(c0 % HALF, c0 % HALF + n)
-            y = ring.tile([P, PACK, n], F32, name="y")
-            per_bank = BANK // n
-            for b in range(PACK // per_bank):
-                bank = psum2.tile([P, per_bank, n], F32, name="y_bank")
-                for i in range(per_bank):
-                    product(bank[:, i, :], w1_w, w1_s, b * per_bank + i, words[:, cols], scales[:, cols])
-                nc.scalar.activation(y[:, b * per_bank : (b + 1) * per_bank, :], bank[:], SIGMOID)
-            return y
+        def pick(name, list_t, tags):
+            words = held([P, S], I32, name + "_words", tags[0])
+            scales = held([P, S], U8, name + "_scales", tags[1])
+            nc.vector.tensor_copy(words[:].bitcast(U32), xw[:].bitcast(U32).indirect(list_t[:]))
+            nc.vector.tensor_copy(scales[:], xs[:].indirect(list_t[:]))
+            return words, scales
 
-        def contacts(k):
-            c0, n, mode = CHUNKS[k]
-            first = ring.tile([P, PACK, n], F32, name="first")
-            second = ring.tile([P, PACK, n], F32, name="second")
-            a = e1_t[:, c0 // 16 : (c0 + n) // 16]
-            b = e2_t[:, c0 // 16 : (c0 + n) // 16]
-            for t in range(PACK):
-                if mode == "V":
-                    nc.vector.tensor_copy(first[:, t, :], c_rows[t][:].indirect(a))
-                else:
-                    nc.scalar.activation(first[:, t, :], u_rows[t][:].indirect(a), SIGMOID)
-                if mode == "S":
-                    nc.scalar.activation(second[:, t, :], u_rows[t][:].indirect(b), SIGMOID)
-            if mode != "S":
-                for t in range(PACK):
-                    nc.vector.tensor_tensor(second[:, t, :], c_rows[t][:].indirect(b), first[:, t, :], ADD)
-            return first, second
+        two_words, two_scales = pick("two", two_t, ("two_w", "two_s"))
+        w2_w = deal_words("w2", w2_rw, "w2_w")
+        w2_s = deal_scales("w2", w2_rs, "w2_s")
 
-        def change(k, y, first, second):
-            c0, n, mode = CHUNKS[k]
-            cols = slice(c0, c0 + n)
-            nc.vector.tensor_tensor(y[:], y[:], rate[:, cols].unsqueeze(1).to_broadcast([P, PACK, n]), MULT)
-            if mode == "S":
-                for t in (0, 2):
-                    nc.vector.tensor_tensor(second[:, t : t + 2, :], second[:, t : t + 2, :], first[:, t : t + 2, :], ADD)
-            for t in range(PACK):
-                nc.vector.scalar_tensor_tensor(second[:, t, :], second[:, t, :], gain[:, t : t + 1], y[:, t, :], MULT, MULT)
-            z = ring.tile([P, PACK, n], BF16, name="z")
-            for t in range(PACK):
-                nc.vector.scalar_tensor_tensor(z[:, t, :], c_rows[t][:, cols], own[:, t : t + 1], second[:, t, :], MULT, ADD)
-            grouped = ring.tile([P, n, PACK], BF16, name="grouped", align_bytes=64)
-            if k == len(CHUNKS) - 1:
-                nc.vector.tensor_copy(grouped[:], z[:].rearrange("p t j -> p j t"))
-            else:
-                nc.scalar.copy(grouped[:], z[:].rearrange("p t j -> p j t"))
-            return grouped
+        own = held([P, PACK], F32, "own")
+        nc.gpsimd.tensor_scalar(own[:], gain[:], -0.75, 0.0, MULT, ADD)
 
-        def layer(k, grouped):
-            c0, n, mode = CHUNKS[k]
-            codes = ring.tile([P, n], I32, name="z_codes", align_bytes=64)
-            scales = ring.tile([P, n], U8, name="z_scales", align_bytes=64)
-            nc.vector.quantize_mx(codes[:].bitcast(FP8X4), scales[:], grouped[:].rearrange("p j t -> p (j t)"))
-            h = ring.tile([P, PACK, n], F32, name="h")
-            per_bank = BANK // n
-            for b in range(PACK // per_bank):
-                bank = psum2.tile([P, per_bank, n], F32, name="h_bank")
-                for i in range(per_bank):
-                    product(bank[:, i, :], w3_w, w3_s, b * per_bank + i, codes[:], scales[:])
-                nc.scalar.copy(h[:, b * per_bank : (b + 1) * per_bank, :], bank[:])
-            return h
-
-        out_rows = out_0.rearrange("(p t) u -> p t u", t=PACK)
-        rounded = keep.tile([P, PACK, U], BF16, name="rounded")
-
-        def put(k, h):
-            c0, n, mode = CHUNKS[k]
-            for t in range(PACK):
-                nc.vector.tensor_copy(pages[t][:].indirect(slot_t[:, c0 // 16 : (c0 + n) // 16]), h[:, t, :])
-                if k == len(CHUNKS) - 1:
-                    nc.sync.dma_start(out_rows[:, t, :], pages[t][:])
-                    if t < PACK - 1:
-                        nc.scalar.copy(rounded[:, t, :], pages[t][:])
-
-        y0 = susceptible(0)
-        first0, second0 = contacts(0)
+        c_banks = [psum.tile([P, BANK], F32, name="c_bank%d" % t, tag="bank%d" % t) for t in range(PACK)]
+        c_rows = [held([P, S], F32, "c_row%d" % t) for t in range(PACK)]
+        u_rows = [held([P, S], F32, "u_row%d" % t) for t in range(PACK)]
+        leave = held([P, PACK, S], F32, "leave")
+        for t in range(PACK):
+            product(c_banks[t][:], w2_w, w2_s, t, two_words[:], two_scales[:])
+            nc.scalar.activation(c_rows[t][:], c_banks[t][:], SIGMOID)
+            nc.gpsimd.tensor_scalar(leave[:, t, :], c_rows[t][:], own[:, t : t + 1], 0.0, MULT, ADD)
         for t in range(PACK):
             nc.scalar.copy(u_rows[t][:], c_banks[t][:])
-        grouped0 = change(0, y0, first0, second0)
-        w3_w = deal_words("w3", w3_rw)
-        w3_s = deal_scales("w3", w3_rs)
-        h_prev = layer(0, grouped0)
-        picked.append(pick("offs1", offs_t, HALF, HALF))
-        for k in range(1, len(CHUNKS)):
-            first, second = contacts(k)
-            y = susceptible(k)
-            grouped = change(k, y, first, second)
-            if k == len(CHUNKS) - 1:
-                h_next = layer(k, grouped)
-                put(k - 1, h_prev)
-            else:
-                put(k - 1, h_prev)
-                h_next = layer(k, grouped)
-            h_prev = h_next
-        put(len(CHUNKS) - 1, h_prev)
 
-        out_codes = keep.tile([P, U], I32, name="out_codes", align_bytes=64)
-        out_scales = keep.tile([P, U], U8, name="out_scales", align_bytes=64)
-        out_words = out_1[0].rearrange("p n t -> p (n t)").bitcast(I32)
+        offs_words, offs_scales = pick("offs", offs_t, ("w2_rs", "w2_rw"))
+        w1_w = deal_words("w1", w1_rw, "two_w")
+        w1_s = deal_scales("w1", w1_rs, "two_s")
+
+        def susceptible(half):
+            cols = slice(half * HALF, (half + 1) * HALF)
+            y = held([P, PACK, HALF], F32, "y%d" % half)
+            for b in range(2):
+                bank = psum.tile([P, 2, HALF], F32, name="y_bank%d_%d" % (half, b))
+                for i in range(2):
+                    product(bank[:, i, :], w1_w, w1_s, 2 * b + i, offs_words[:, cols], offs_scales[:, cols])
+                nc.scalar.activation(y[:, 2 * b : 2 * b + 2, :], bank[:], SIGMOID)
+            return y
+
+        def exposure(half, y):
+            exposed = held([P, PACK, HALF], F32, "exposed%d" % half)
+            for t in range(PACK):
+                nc.vector.scalar_tensor_tensor(
+                    exposed[:, t, :], y[:, t, :], gain[:, t : t + 1], rate[:, half * HALF : (half + 1) * HALF], MULT, MULT
+                )
+            return exposed
+
+        def contacts_on_vector(k):
+            first = held([P, PACK, CHUNK], F32, "first%d" % k)
+            both = held([P, PACK, CHUNK], F32, "both%d" % k)
+            for t in range(PACK):
+                nc.vector.tensor_copy(first[:, t, :], c_rows[t][:].indirect(entries(e1_t, k * CHUNK, CHUNK)))
+            for t in range(PACK):
+                nc.vector.tensor_tensor(both[:, t, :], c_rows[t][:].indirect(entries(e2_t, k * CHUNK, CHUNK)), first[:, t, :], ADD)
+            return [both[:, :, a * SUB : (a + 1) * SUB] for a in range(CHUNK // SUB)]
+
+        def contacts_on_scalar(k):
+            pair = held([P, 2, PACK, CHUNK], F32, "pair%d" % k)
+            for t in range(PACK):
+                nc.scalar.activation(pair[:, 0, t, :], u_rows[t][:].indirect(entries(e1_t, k * CHUNK, CHUNK)), SIGMOID)
+                nc.scalar.activation(pair[:, 1, t, :], u_rows[t][:].indirect(entries(e2_t, k * CHUNK, CHUNK)), SIGMOID)
+            return pair
+
+        def contact_sums(k, pair):
+            sums = []
+            for a in range(CHUNK // SUB):
+                both = held([P, PACK, SUB], F32, "both%d_%d" % (k, a))
+                cols = slice(a * SUB, (a + 1) * SUB)
+                nc.vector.tensor_tensor(both[:], pair[:, 0, :, cols], pair[:, 1, :, cols], ADD)
+                sums.append(both[:])
+            return sums
+
+        def change(k, exposed, sums):
+            fresh = []
+            for a in range(CHUNK // SUB):
+                c0 = (k * CHUNK) % HALF + a * SUB
+                cases = held([P, PACK, SUB], F32, "cases%d_%d" % (k, a))
+                nc.vector.tensor_tensor(cases[:], sums[a], exposed[:, :, c0 : c0 + SUB], MULT)
+                fresh.append(cases)
+            grouped = held([P, CHUNK, PACK], BF16, "grouped%d" % k)
+            for a in range(CHUNK // SUB):
+                c0 = k * CHUNK + a * SUB
+                nc.vector.tensor_tensor(
+                    grouped[:, a * SUB : (a + 1) * SUB, :].rearrange("p (c i) t -> p c t i", i=4),
+                    fresh[a][:].rearrange("p t (c i) -> p c t i", i=4),
+                    leave[:, :, c0 : c0 + SUB].rearrange("p t (c i) -> p c t i", i=4),
+                    ADD,
+                )
+            codes = held([P, CHUNK], I32, "z_codes%d" % k)
+            scales = held([P, CHUNK], U8, "z_scales%d" % k)
+            nc.vector.quantize_mx(codes[:].bitcast(FP8X4), scales[:], grouped[:].rearrange("p j t -> p (j t)"))
+            bank = psum.tile([P, PACK, CHUNK], F32, name="h_bank%d" % k, tag="bank%d" % k)
+            for t in range(PACK):
+                product(bank[:, t, :], w3_w, w3_s, t, codes[:], scales[:])
+            return bank
+
+        y0 = susceptible(0)
+        sums0 = contacts_on_vector(0)
+        pair1 = contacts_on_scalar(1)
+        y1 = susceptible(1)
+        pair2 = contacts_on_scalar(2)
+        pair3 = contacts_on_scalar(3)
+        exposed0 = exposure(0, y0)
+        w3_w = deal_words("w3", w3_rw, "w3_w")
+        w3_s = deal_scales("w3", w3_rs, "w3_s")
+        banks = [change(0, exposed0, sums0)]
+        banks.append(change(1, exposed0, contact_sums(1, pair1)))
+        exposed1 = exposure(1, y1)
+        banks.append(change(2, exposed1, contact_sums(2, pair2)))
+        banks.append(change(3, exposed1, contact_sums(3, pair3)))
+
+        h = held([P, PACK, S], F32, "h")
+        for k in range(S // CHUNK):
+            nc.scalar.copy(h[:, :, k * CHUNK : (k + 1) * CHUNK], banks[k][:])
+
+        out_rows = out_0.rearrange("(p t) u -> p t u", t=PACK)
+        blocks = [held([P, PIECE, PACK], BF16, "block%d" % i) for i in range(U // PIECE)]
         last = PACK - 1
-        blocks = []
-        for i, (c0, n, engine) in enumerate(TAIL):
-            cols = slice(c0, c0 + n)
-            block = keep.tile([P, n, PACK], BF16, name="block%d" % i, align_bytes=64)
-            source = rounded[:, :, cols].rearrange("p t j -> p j t")
-            if engine == "V":
-                nc.vector.tensor_copy(rounded[:, last, cols], pages[last][:, cols])
-                nc.vector.tensor_copy(block[:], source)
+        on_vector = 2
+        for t in range(PACK):
+            if t == 0:
+                early = S - CHUNK
+                nc.vector.tensor_copy(pages[t][:].indirect(entries(slot_t, 0, early)), h[:, t, 0:early])
+                nc.vector.tensor_copy(pages[t][:].indirect(entries(slot_t, early, CHUNK)), h[:, t, early:S])
             else:
-                nc.scalar.copy(rounded[:, last, cols], pages[last][:, cols])
-                nc.scalar.copy(block[:], source)
-            blocks.append(block)
-        for i, (c0, n, engine) in enumerate(TAIL):
-            cols = slice(c0, c0 + n)
+                nc.vector.tensor_copy(pages[t][:].indirect(slot_t[:]), h[:, t, :])
+            nc.sync.dma_start(out_rows[:, t, :], pages[t][:])
+            for i in range(U // PIECE):
+                source = pages[t][:, i * PIECE : (i + 1) * PIECE]
+                if t == last and i < on_vector:
+                    nc.vector.tensor_copy(blocks[i][:, :, t], source)
+                elif t == last - 1 and i < on_vector:
+                    nc.scalar.copy(blocks[i][:, :, t : t + 2], source.unsqueeze(2).to_broadcast([P, PIECE, 2]))
+                else:
+                    nc.scalar.copy(blocks[i][:, :, t], source)
+
+        out_codes = held([P, U], I32, "out_codes")
+        out_scales = held([P, U], U8, "out_scales")
+        out_words = out_1[0].rearrange("p n t -> p (n t)").bitcast(I32)
+        for i in range(U // PIECE):
+            cols = slice(i * PIECE, (i + 1) * PIECE)
             nc.vector.quantize_mx(out_codes[:, cols].bitcast(FP8X4), out_scales[:, cols], blocks[i][:].rearrange("p j t -> p (j t)"))
-            nc.sync.dma_start(out_words[:, cols], out_codes[:, cols])
+            if i % 2 == 1:
+                both = slice((i - 1) * PIECE, (i + 1) * PIECE)
+                nc.sync.dma_start(out_words[:, both], out_codes[:, both])
         for q in range(4):
             queue = nc.sync if q % 2 == 0 else nc.scalar
             queue.dma_start(out_2[0, 4 * q : 4 * q + 4, :].bitcast(I32), out_scales[32 * q : 32 * q + 4, :].bitcast(I32))

@@ -22,9 +22,10 @@ P = 128
 PACK = 4
 BANK = 512
 CHUNK = 128
-HALF = 256
+ON_VECTOR = 192
 SUB = 64
-PIECE = 256
+BLOCKS = [(0, 512), (512, 256), (768, 256)]
+ROUNDED_ON_VECTOR = 512
 
 
 def tile_picked_sirstep_none_po_kernel(
@@ -86,8 +87,9 @@ def tile_picked_sirstep_none_po_kernel(
             return list_t[:, c0 // 16 : (c0 + n) // 16]
 
         xs = held([P, T], U8, "xs")
-        nc.vector.memset(xs[:].bitcast(I32), 0)
+        nc.gpsimd.memset(xs[:].bitcast(I32), 0)
         two_t = load_list("two_t", two)
+        offs_t = load_list("offs_t", offs)
         w2_rw, w2_rs = raw_weight("w2", w2_words, ("w2_rw", "w2_rs"))
         load_scale_rows(xs, x_scales, (nc.sync,) * 4)
         xw = held([P, T], I32, "xw")
@@ -98,8 +100,7 @@ def tile_picked_sirstep_none_po_kernel(
         warm_out = held([P, 1], F32, "warm_out")
         nc.gpsimd.memset(warm[:], 0.0)
         nc.scalar.activation(warm_out[:], warm[:], SIGMOID)
-        offs_t = load_list("offs_t", offs)
-        w1_rw, w1_rs = raw_weight("w1", w1_words, ("w1_rw", "w1_rs"))
+        w1_rw, w1_rs = raw_weight("w1", w1_words, ("page0", "page2"))
         e1_t = load_list("e1_t", e1)
         e2_t = load_list("e2_t", e2)
         gain = held([P, PACK], F32, "gain")
@@ -108,16 +109,10 @@ def tile_picked_sirstep_none_po_kernel(
         load_scale_rows(w1_rs, w1_scales, (nc.gpsimd,) * 4)
         rate = held([P, S], F32, "rate")
         nc.sync.dma_start(rate[:], beta.rearrange("(p t) s -> p t s", t=PACK)[:, 0, :])
-        w3_rw, w3_rs = raw_weight("w3", w3_words, ("w3_rw", "w3_rs"))
+        w3_rw, w3_rs = raw_weight("w3", w3_words, ("page1", "page3"))
         nc.vector.memset(w3_rs[:].bitcast(I32), 0)
         load_scale_rows(w3_rs, w3_scales, (nc.sync,) * 4)
         slot_t = load_list("slot_t", slot)
-        mem_rows = mem.rearrange("(p t) u -> p t u", t=PACK)
-        pages = []
-        for t in range(PACK):
-            page = held([P, U], F32, "page%d" % t)
-            nc.sync.dma_start(page[:], mem_rows[:, t, :])
-            pages.append(page)
 
         def pick(name, list_t, tags):
             words = held([P, S], I32, name + "_words", tags[0])
@@ -148,65 +143,56 @@ def tile_picked_sirstep_none_po_kernel(
         w1_w = deal_words("w1", w1_rw, "two_w")
         w1_s = deal_scales("w1", w1_rs, "two_s")
 
-        def susceptible(half):
-            cols = slice(half * HALF, (half + 1) * HALF)
-            y = held([P, PACK, HALF], F32, "y%d" % half)
-            for b in range(2):
-                bank = psum.tile([P, 2, HALF], F32, name="y_bank%d_%d" % (half, b))
-                for i in range(2):
-                    product(bank[:, i, :], w1_w, w1_s, 2 * b + i, offs_words[:, cols], offs_scales[:, cols])
-                nc.scalar.activation(y[:, 2 * b : 2 * b + 2, :], bank[:], SIGMOID)
-            return y
+        y = held([P, PACK, S], F32, "y")
+        for t in range(PACK):
+            bank = psum.tile([P, BANK], F32, name="y_bank%d" % t)
+            product(bank[:], w1_w, w1_s, t, offs_words[:], offs_scales[:])
+            nc.scalar.activation(y[:, t, :], bank[:], SIGMOID)
 
-        def exposure(half, y):
-            exposed = held([P, PACK, HALF], F32, "exposed%d" % half)
-            for t in range(PACK):
-                nc.vector.scalar_tensor_tensor(
-                    exposed[:, t, :], y[:, t, :], gain[:, t : t + 1], rate[:, half * HALF : (half + 1) * HALF], MULT, MULT
-                )
-            return exposed
+        both = held([P, PACK, S], F32, "both")
+        first = held([P, PACK, ON_VECTOR], F32, "first")
+        for t in range(PACK):
+            nc.vector.tensor_copy(first[:, t, :], c_rows[t][:].indirect(entries(e1_t, 0, ON_VECTOR)))
+        for t in range(PACK):
+            nc.vector.tensor_tensor(both[:, t, 0:ON_VECTOR], c_rows[t][:].indirect(entries(e2_t, 0, ON_VECTOR)), first[:, t, :], ADD)
 
-        def contacts_on_vector(k):
-            first = held([P, PACK, CHUNK], F32, "first%d" % k)
-            both = held([P, PACK, CHUNK], F32, "both%d" % k)
+        def contacts_on_scalar(name, c0, n):
+            pair = held([P, 2, PACK, n], F32, name)
             for t in range(PACK):
-                nc.vector.tensor_copy(first[:, t, :], c_rows[t][:].indirect(entries(e1_t, k * CHUNK, CHUNK)))
-            for t in range(PACK):
-                nc.vector.tensor_tensor(both[:, t, :], c_rows[t][:].indirect(entries(e2_t, k * CHUNK, CHUNK)), first[:, t, :], ADD)
-            return [both[:, :, a * SUB : (a + 1) * SUB] for a in range(CHUNK // SUB)]
-
-        def contacts_on_scalar(k):
-            pair = held([P, 2, PACK, CHUNK], F32, "pair%d" % k)
-            for t in range(PACK):
-                nc.scalar.activation(pair[:, 0, t, :], u_rows[t][:].indirect(entries(e1_t, k * CHUNK, CHUNK)), SIGMOID)
-                nc.scalar.activation(pair[:, 1, t, :], u_rows[t][:].indirect(entries(e2_t, k * CHUNK, CHUNK)), SIGMOID)
+                nc.scalar.activation(pair[:, 0, t, :], u_rows[t][:].indirect(entries(e1_t, c0, n)), SIGMOID)
+                nc.scalar.activation(pair[:, 1, t, :], u_rows[t][:].indirect(entries(e2_t, c0, n)), SIGMOID)
             return pair
 
-        def contact_sums(k, pair):
-            sums = []
-            for a in range(CHUNK // SUB):
-                both = held([P, PACK, SUB], F32, "both%d_%d" % (k, a))
-                cols = slice(a * SUB, (a + 1) * SUB)
-                nc.vector.tensor_tensor(both[:], pair[:, 0, :, cols], pair[:, 1, :, cols], ADD)
-                sums.append(both[:])
-            return sums
+        LATE = S - CHUNK
+        wide = contacts_on_scalar("wide", ON_VECTOR, LATE - ON_VECTOR)
+        late = contacts_on_scalar("late", LATE, CHUNK)
 
-        def change(k, exposed, sums):
-            fresh = []
-            for a in range(CHUNK // SUB):
-                c0 = (k * CHUNK) % HALF + a * SUB
-                cases = held([P, PACK, SUB], F32, "cases%d_%d" % (k, a))
-                nc.vector.tensor_tensor(cases[:], sums[a], exposed[:, :, c0 : c0 + SUB], MULT)
-                fresh.append(cases)
-            grouped = held([P, CHUNK, PACK], BF16, "grouped%d" % k)
-            for a in range(CHUNK // SUB):
-                c0 = k * CHUNK + a * SUB
-                nc.vector.tensor_tensor(
-                    grouped[:, a * SUB : (a + 1) * SUB, :].rearrange("p (c i) t -> p c t i", i=4),
-                    fresh[a][:].rearrange("p t (c i) -> p c t i", i=4),
-                    leave[:, :, c0 : c0 + SUB].rearrange("p t (c i) -> p c t i", i=4),
-                    ADD,
-                )
+        w3_w = deal_words("w3", w3_rw, "w3_w")
+        w3_s = deal_scales("w3", w3_rs, "w3_s")
+        mem_rows = mem.rearrange("(p t) u -> p t u", t=PACK)
+        pages = []
+        for t in range(PACK):
+            page = held([P, U], F32, "page%d" % t)
+            nc.sync.dma_start(page[:], mem_rows[:, t, :])
+            pages.append(page)
+        exposed = held([P, PACK, S], F32, "exposed")
+        for t in range(PACK):
+            nc.vector.scalar_tensor_tensor(exposed[:, t, :], y[:, t, :], gain[:, t : t + 1], rate[:], MULT, MULT)
+
+        cases = held([P, PACK, S], F32, "cases")
+
+        def new_cases(rows, cols):
+            nc.vector.tensor_tensor(cases[:, rows, cols], both[:, rows, cols], exposed[:, rows, cols], MULT)
+
+        def change(grouped, c0, n):
+            nc.vector.tensor_tensor(
+                grouped[:, c0 % CHUNK : c0 % CHUNK + n, :].rearrange("p (c i) t -> p c t i", i=4),
+                cases[:, :, c0 : c0 + n].rearrange("p t (c i) -> p c t i", i=4),
+                leave[:, :, c0 : c0 + n].rearrange("p t (c i) -> p c t i", i=4),
+                ADD,
+            )
+
+        def layer(k, grouped):
             codes = held([P, CHUNK], I32, "z_codes%d" % k)
             scales = held([P, CHUNK], U8, "z_scales%d" % k)
             nc.vector.quantize_mx(codes[:].bitcast(FP8X4), scales[:], grouped[:].rearrange("p j t -> p (j t)"))
@@ -215,55 +201,57 @@ def tile_picked_sirstep_none_po_kernel(
                 product(bank[:, t, :], w3_w, w3_s, t, codes[:], scales[:])
             return bank
 
-        y0 = susceptible(0)
-        sums0 = contacts_on_vector(0)
-        pair1 = contacts_on_scalar(1)
-        y1 = susceptible(1)
-        pair2 = contacts_on_scalar(2)
-        pair3 = contacts_on_scalar(3)
-        exposed0 = exposure(0, y0)
-        w3_w = deal_words("w3", w3_rw, "w3_w")
-        w3_s = deal_scales("w3", w3_rs, "w3_s")
-        banks = [change(0, exposed0, sums0)]
-        banks.append(change(1, exposed0, contact_sums(1, pair1)))
-        exposed1 = exposure(1, y1)
-        banks.append(change(2, exposed1, contact_sums(2, pair2)))
-        banks.append(change(3, exposed1, contact_sums(3, pair3)))
+        z = [held([P, CHUNK, PACK], BF16, "z%d" % k) for k in range(S // CHUNK)]
+        new_cases(slice(0, PACK), slice(0, CHUNK))
+        change(z[0], 0, CHUNK)
+        for t in range(PACK):
+            nc.vector.tensor_tensor(both[:, t, ON_VECTOR:LATE], wide[:, 0, t, :], wide[:, 1, t, :], ADD)
+            if t == 0:
+                banks = [layer(0, z[0])]
+            if t % 2 == 1:
+                new_cases(slice(t - 1, t + 1), slice(CHUNK, LATE))
+        change(z[1], CHUNK, CHUNK)
+        change(z[2], 2 * CHUNK, CHUNK)
+        banks.append(layer(1, z[1]))
+        banks.append(layer(2, z[2]))
+        for t in (0, 2):
+            nc.vector.tensor_tensor(both[:, t : t + 2, LATE:S], late[:, 0, t : t + 2, :], late[:, 1, t : t + 2, :], ADD)
+            new_cases(slice(t, t + 2), slice(LATE, S))
+        change(z[3], LATE, SUB)
+        change(z[3], LATE + SUB, SUB)
+        banks.append(layer(3, z[3]))
 
         h = held([P, PACK, S], F32, "h")
         for k in range(S // CHUNK):
             nc.scalar.copy(h[:, :, k * CHUNK : (k + 1) * CHUNK], banks[k][:])
 
         out_rows = out_0.rearrange("(p t) u -> p t u", t=PACK)
-        blocks = [held([P, PIECE, PACK], BF16, "block%d" % i) for i in range(U // PIECE)]
+        blocks = [held([P, n, PACK], BF16, "block%d" % c0) for c0, n in BLOCKS]
         last = PACK - 1
-        on_vector = 2
         for t in range(PACK):
             if t == 0:
-                early = S - CHUNK
-                nc.vector.tensor_copy(pages[t][:].indirect(entries(slot_t, 0, early)), h[:, t, 0:early])
-                nc.vector.tensor_copy(pages[t][:].indirect(entries(slot_t, early, CHUNK)), h[:, t, early:S])
+                nc.vector.tensor_copy(pages[t][:].indirect(entries(slot_t, 0, LATE)), h[:, t, 0:LATE])
+                nc.vector.tensor_copy(pages[t][:].indirect(entries(slot_t, LATE, CHUNK)), h[:, t, LATE:S])
             else:
                 nc.vector.tensor_copy(pages[t][:].indirect(slot_t[:]), h[:, t, :])
             nc.sync.dma_start(out_rows[:, t, :], pages[t][:])
-            for i in range(U // PIECE):
-                source = pages[t][:, i * PIECE : (i + 1) * PIECE]
-                if t == last and i < on_vector:
-                    nc.vector.tensor_copy(blocks[i][:, :, t], source)
-                elif t == last - 1 and i < on_vector:
-                    nc.scalar.copy(blocks[i][:, :, t : t + 2], source.unsqueeze(2).to_broadcast([P, PIECE, 2]))
+            for block, (c0, n) in zip(blocks, BLOCKS):
+                source = pages[t][:, c0 : c0 + n]
+                if t == last and c0 < ROUNDED_ON_VECTOR:
+                    nc.vector.tensor_copy(block[:, :, t], source)
+                elif t == last - 1 and c0 < ROUNDED_ON_VECTOR:
+                    nc.scalar.copy(block[:, :, t : t + 2], source.unsqueeze(2).to_broadcast([P, n, 2]))
                 else:
-                    nc.scalar.copy(blocks[i][:, :, t], source)
+                    nc.scalar.copy(block[:, :, t], source)
 
         out_codes = held([P, U], I32, "out_codes")
         out_scales = held([P, U], U8, "out_scales")
         out_words = out_1[0].rearrange("p n t -> p (n t)").bitcast(I32)
-        for i in range(U // PIECE):
-            cols = slice(i * PIECE, (i + 1) * PIECE)
-            nc.vector.quantize_mx(out_codes[:, cols].bitcast(FP8X4), out_scales[:, cols], blocks[i][:].rearrange("p j t -> p (j t)"))
-            if i % 2 == 1:
-                both = slice((i - 1) * PIECE, (i + 1) * PIECE)
-                nc.sync.dma_start(out_words[:, both], out_codes[:, both])
+
+        for block, (c0, n) in zip(blocks, BLOCKS):
+            cols = slice(c0, c0 + n)
+            nc.vector.quantize_mx(out_codes[:, cols].bitcast(FP8X4), out_scales[:, cols], block[:].rearrange("p j t -> p (j t)"))
+            nc.sync.dma_start(out_words[:, cols], out_codes[:, cols])
         for q in range(4):
             queue = nc.sync if q % 2 == 0 else nc.scalar
             queue.dma_start(out_2[0, 4 * q : 4 * q + 4, :].bitcast(I32), out_scales[32 * q : 32 * q + 4, :].bitcast(I32))

from contextlib import ExitStack

import concourse.mybir as mybir

K, T, S, N, H, U = 512, 2048, 512, 512, 512, 1024
FLOPS = 3 * 2 * 512 * 512 * 512

F32 = mybir.dt.float32
BF16 = mybir.dt.bfloat16
I32 = mybir.dt.int32
U32 = mybir.dt.uint32
U16 = mybir.dt.uint16
U8 = mybir.dt.uint8
FP8X4 = mybir.dt.float8_e4m3fn_x4
FP4X4 = mybir.dt.float4_e2m1fn_x4
MULT = mybir.AluOpType.mult
ADD = mybir.AluOpType.add
SIGMOID = mybir.ActivationFunctionType.Sigmoid
COPY = mybir.ActivationFunctionType.Copy

P = 128
PACK = 4
BANK = 512
CHUNK = 128
ON_VECTOR = 192
SUB = 64
BLOCKS = [(0, 512), (512, 256), (768, 256)]
ROUNDED_ON_VECTOR = 512


def tile_picked_sirstep_none_po_kernel(
    tc, x_words, x_scales, w1_words, w1_scales, w2_words, w2_scales, beta, gn, w3_words, w3_scales,
    mem, offs, two, e1, e2, slot, out_0, out_1, out_2,
):
    nc = tc.nc
    with ExitStack() as ctx:
        lists = ctx.enter_context(tc.tile_pool(name="lists", bufs=1))
        keep = ctx.enter_context(tc.tile_pool(name="keep", bufs=1))
        psum = ctx.enter_context(tc.psum_pool(name="psum", bufs=1))

        def load_list(name, src):
            tile = lists.tile([P, S // 16], U16, name=name)
            nc.sync.dma_start(tile[:], src)
            return tile

        def load_scale_rows(tile, src, queues):
            for q in range(4):
                queues[q].dma_start(tile[32 * q : 32 * q + 4, :].bitcast(I32), src[0, 4 * q : 4 * q + 4, :].bitcast(I32))

        def raw_weight(name, words, tags):
            raw_words = keep.tile([P, 2 * H], U8, name=name + "_raw_words", tag=tags[0], align_bytes=64)
            raw_scales = keep.tile([P, H], U8, name=name + "_raw_scales", tag=tags[1], align_bytes=64)
            nc.sync.dma_start(raw_words[:].bitcast(I32), words[0].bitcast(I32))
            return raw_words, raw_scales

        def deal_words(name, raw_words, tag):
            dealt = keep.tile([P, 2 * H], U8, name=name + "_words", tag=tag, align_bytes=64)
            nc.vector.tensor_copy(
                dealt[:].rearrange("p (t m b) -> p m t b", t=PACK, b=2),
                raw_words[:].rearrange("p (m t b) -> p m t b", t=PACK, b=2),
            )
            return dealt

        def deal_scales(name, raw_scales, tag):
            dealt = keep.tile([P, H], U8, name=name + "_scales", tag=tag, align_bytes=64)
            nc.vector.tensor_copy(
                dealt[:].rearrange("p (t m) -> p m t", t=PACK),
                raw_scales[:].rearrange("p (m t) -> p m t", t=PACK),
            )
            return dealt

        def product(out, w_words, w_scales, t, codes, scales):
            nc.tensor.matmul_mx(
                out,
                lhsT=w_words[:, 2 * P * t : 2 * P * (t + 1)].bitcast(FP4X4),
                lhsT_scale=w_scales[:, P * t : P * (t + 1)],
                rhs=codes.bitcast(FP8X4),
                rhs_scale=scales,
                start=True,
                stop=True,
            )

        def held(shape, dtype, name, tag=None):
            return keep.tile(shape, dtype, name=name, tag=tag or name, align_bytes=64)

        def entries(list_t, c0, n):
            return list_t[:, c0 // 16 : (c0 + n) // 16]

        xs = held([P, T], U8, "xs")
        nc.gpsimd.memset(xs[:].bitcast(I32), 0)
        two_t = load_list("two_t", two)
        offs_t = load_list("offs_t", offs)
        w2_rw, w2_rs = raw_weight("w2", w2_words, ("w2_rw", "w2_rs"))
        load_scale_rows(xs, x_scales, (nc.sync,) * 4)
        xw = held([P, T], I32, "xw")
        nc.sync.dma_start(xw[:], x_words[0].rearrange("p n t -> p (n t)").bitcast(I32))
        nc.vector.memset(w2_rs[:].bitcast(I32), 0)
        load_scale_rows(w2_rs, w2_scales, (nc.sync,) * 4)
        warm = held([P, 1], F32, "warm")
        warm_out = held([P, 1], F32, "warm_out")
        nc.gpsimd.memset(warm[:], 0.0)
        nc.scalar.activation(warm_out[:], warm[:], SIGMOID)
        w1_rw, w1_rs = raw_weight("w1", w1_words, ("page0", "page2"))
        e1_t = load_list("e1_t", e1)
        e2_t = load_list("e2_t", e2)
        gain = held([P, PACK], F32, "gain")
        nc.sync.dma_start(gain[:], gn.rearrange("(p t) o -> p (t o)", t=PACK))
        nc.gpsimd.memset(w1_rs[:].bitcast(I32), 0)
        load_scale_rows(w1_rs, w1_scales, (nc.gpsimd,) * 4)
        rate = held([P, S], F32, "rate")
        nc.sync.dma_start(rate[:], beta.rearrange("(p t) s -> p t s", t=PACK)[:, 0, :])
        w3_rw, w3_rs = raw_weight("w3", w3_words, ("page1", "page3"))
        nc.vector.memset(w3_rs[:].bitcast(I32), 0)
        load_scale_rows(w3_rs, w3_scales, (nc.sync,) * 4)
        slot_t = load_list("slot_t", slot)

        def pick(name, list_t, tags):
            words = held([P, S], I32, name + "_words", tags[0])
            scales = held([P, S], U8, name + "_scales", tags[1])
            nc.vector.tensor_copy(words[:].bitcast(U32), xw[:].bitcast(U32).indirect(list_t[:]))
            nc.vector.tensor_copy(scales[:], xs[:].indirect(list_t[:]))
            return words, scales

        two_words, two_scales = pick("two", two_t, ("two_w", "two_s"))
        w2_w = deal_words("w2", w2_rw, "w2_w")
        w2_s = deal_scales("w2", w2_rs, "w2_s")

        own = held([P, PACK], F32, "own")
        nc.gpsimd.tensor_scalar(own[:], gain[:], -0.75, 0.0, MULT, ADD)

        c_banks = [psum.tile([P, BANK], F32, name="c_bank%d" % t, tag="bank%d" % t) for t in range(PACK)]
        c_rows = [held([P, S], F32, "c_row%d" % t) for t in range(PACK)]
        u_rows = [held([P, S], F32, "u_row%d" % t) for t in range(PACK)]
        leave = held([P, PACK, S], F32, "leave")
        for t in range(PACK):
            product(c_banks[t][:], w2_w, w2_s, t, two_words[:], two_scales[:])
            nc.scalar.activation(c_rows[t][:], c_banks[t][:], SIGMOID)
            nc.gpsimd.tensor_scalar(leave[:, t, :], c_rows[t][:], own[:, t : t + 1], 0.0, MULT, ADD)
        for t in range(PACK):
            nc.scalar.copy(u_rows[t][:], c_banks[t][:])

        offs_words, offs_scales = pick("offs", offs_t, ("w2_rs", "w2_rw"))
        w1_w = deal_words("w1", w1_rw, "two_w")
        w1_s = deal_scales("w1", w1_rs, "two_s")

        y = held([P, PACK, S], F32, "y")
        for t in range(PACK):
            bank = psum.tile([P, BANK], F32, name="y_bank%d" % t)
            product(bank[:], w1_w, w1_s, t, offs_words[:], offs_scales[:])
            nc.scalar.activation(y[:, t, :], bank[:], SIGMOID)

        both = held([P, PACK, S], F32, "both")
        first = held([P, PACK, ON_VECTOR], F32, "first")
        for t in range(PACK):
            nc.vector.tensor_copy(first[:, t, :], c_rows[t][:].indirect(entries(e1_t, 0, ON_VECTOR)))
        for t in range(PACK):
            nc.vector.tensor_tensor(both[:, t, 0:ON_VECTOR], c_rows[t][:].indirect(entries(e2_t, 0, ON_VECTOR)), first[:, t, :], ADD)

        def contacts_on_scalar(name, c0, n):
            pair = held([P, 2, PACK, n], F32, name)
            for t in range(PACK):
                nc.scalar.activation(pair[:, 0, t, :], u_rows[t][:].indirect(entries(e1_t, c0, n)), SIGMOID)
                nc.scalar.activation(pair[:, 1, t, :], u_rows[t][:].indirect(entries(e2_t, c0, n)), SIGMOID)
            return pair

        LATE = S - CHUNK
        wide = contacts_on_scalar("wide", ON_VECTOR, LATE - ON_VECTOR)
        late = contacts_on_scalar("late", LATE, CHUNK)

        w3_w = deal_words("w3", w3_rw, "w3_w")
        w3_s = deal_scales("w3", w3_rs, "w3_s")
        mem_rows = mem.rearrange("(p t) u -> p t u", t=PACK)
        pages = []
        for t in range(PACK):
            page = held([P, U], F32, "page%d" % t)
            nc.sync.dma_start(page[:], mem_rows[:, t, :])
            pages.append(page)
        exposed = held([P, PACK, S], F32, "exposed")
        for t in range(PACK):
            nc.vector.scalar_tensor_tensor(exposed[:, t, :], y[:, t, :], gain[:, t : t + 1], rate[:], MULT, MULT)

        cases = held([P, PACK, S], F32, "cases")

        def new_cases(rows, cols):
            nc.vector.tensor_tensor(cases[:, rows, cols], both[:, rows, cols], exposed[:, rows, cols], MULT)

        def change(grouped, c0, n):
            nc.vector.tensor_tensor(
                grouped[:, c0 % CHUNK : c0 % CHUNK + n, :].rearrange("p (c i) t -> p c t i", i=4),
                cases[:, :, c0 : c0 + n].rearrange("p t (c i) -> p c t i", i=4),
                leave[:, :, c0 : c0 + n].rearrange("p t (c i) -> p c t i", i=4),
                ADD,
            )

        def layer(k, grouped):
            codes = held([P, CHUNK], I32, "z_codes%d" % k)
            scales = held([P, CHUNK], U8, "z_scales%d" % k)
            nc.vector.quantize_mx(codes[:].bitcast(FP8X4), scales[:], grouped[:].rearrange("p j t -> p (j t)"))
            bank = psum.tile([P, PACK, CHUNK], F32, name="h_bank%d" % k, tag="bank%d" % k)
            for t in range(PACK):
                product(bank[:, t, :], w3_w, w3_s, t, codes[:], scales[:])
            return bank

        z = [held([P, CHUNK, PACK], BF16, "z%d" % k) for k in range(S // CHUNK)]
        new_cases(slice(0, PACK), slice(0, CHUNK))
        change(z[0], 0, CHUNK)
        for t in range(PACK):
            nc.vector.tensor_tensor(both[:, t, ON_VECTOR:LATE], wide[:, 0, t, :], wide[:, 1, t, :], ADD)
            if t == 0:
                banks = [layer(0, z[0])]
            if t % 2 == 1:
                new_cases(slice(t - 1, t + 1), slice(CHUNK, LATE))
        change(z[1], CHUNK, CHUNK)
        change(z[2], 2 * CHUNK, CHUNK)
        banks.append(layer(1, z[1]))
        banks.append(layer(2, z[2]))
        for t in (0, 2):
            nc.vector.tensor_tensor(both[:, t : t + 2, LATE:S], late[:, 0, t : t + 2, :], late[:, 1, t : t + 2, :], ADD)
            new_cases(slice(t, t + 2), slice(LATE, S))
        change(z[3], LATE, SUB)
        change(z[3], LATE + SUB, SUB)
        banks.append(layer(3, z[3]))

        h = held([P, PACK, S], F32, "h")
        for k in range(S // CHUNK):
            nc.scalar.copy(h[:, :, k * CHUNK : (k + 1) * CHUNK], banks[k][:])

        out_rows = out_0.rearrange("(p t) u -> p t u", t=PACK)
        blocks = [held([P, n, PACK], BF16, "block%d" % c0) for c0, n in BLOCKS]
        last = PACK - 1
        for t in range(PACK):
            if t == 0:
                nc.vector.tensor_copy(pages[t][:].indirect(entries(slot_t, 0, LATE)), h[:, t, 0:LATE])
                nc.vector.tensor_copy(pages[t][:].indirect(entries(slot_t, LATE, CHUNK)), h[:, t, LATE:S])
            else:
                nc.vector.tensor_copy(pages[t][:].indirect(slot_t[:]), h[:, t, :])
            nc.sync.dma_start(out_rows[:, t, :], pages[t][:])
            for block, (c0, n) in zip(blocks, BLOCKS):
                source = pages[t][:, c0 : c0 + n]
                if t == last and c0 < ROUNDED_ON_VECTOR:
                    nc.vector.tensor_copy(block[:, :, t], source)
                elif t == last - 1 and c0 < ROUNDED_ON_VECTOR:
                    nc.scalar.copy(block[:, :, t : t + 2], source.unsqueeze(2).to_broadcast([P, n, 2]))
                else:
                    nc.scalar.copy(block[:, :, t], source)

        out_codes = held([P, U], I32, "out_codes")
        out_scales = held([P, U], U8, "out_scales")
        out_words = out_1[0].rearrange("p n t -> p (n t)").bitcast(I32)

        for block, (c0, n) in zip(blocks, BLOCKS):
            cols = slice(c0, c0 + n)
            nc.vector.quantize_mx(out_codes[:, cols].bitcast(FP8X4), out_scales[:, cols], block[:].rearrange("p j t -> p (j t)"))
            nc.sync.dma_start(out_words[:, cols], out_codes[:, cols])
        for q in range(4):
            queue = nc.sync if q % 2 == 0 else nc.scalar
            queue.dma_start(out_2[0, 4 * q : 4 * q + 4, :].bitcast(I32), out_scales[32 * q : 32 * q + 4, :].bitcast(I32))
